import numpy as np
import ml_dtypes


def mxq(x, axis, fmt="e4m3"):
    dtype, down = {"e4m3": (ml_dtypes.float8_e4m3fn, 7), "e5m2": (ml_dtypes.float8_e5m2, 14)}[fmt]
    v = np.moveaxis(np.asarray(x, np.float32).astype(ml_dtypes.bfloat16).astype(np.float64), axis, -1)
    blocks = v.reshape(v.shape[:-1] + (-1, 32))
    amax = np.abs(blocks).max(-1, keepdims=True)
    byte = np.maximum(np.where(amax > 0, np.frexp(amax)[1] - 1 + 127, 0) - down, 1)
    scale = np.exp2(byte - 127.0)
    codes = (blocks / scale).astype(np.float32).astype(dtype).astype(np.float64)
    return np.moveaxis((codes * scale).reshape(v.shape), -1, axis)


WIDE = False


def mx_kscale(k):
    if not WIDE:
        return np.ones(k)
    levels = np.array([10, -10, 5, -5, 0])
    if k % 512:
        return np.exp2(np.random.permutation(np.resize(levels, k // 32))).repeat(32)
    a = np.empty((k // 512, 16))
    for p in range(k // 512):
        a[p, :8] = np.random.permutation(np.resize(levels, 8))
        for g in range(8):
            far = levels[np.abs(levels - a[p, g]) >= 10]
            a[p, g + 8] = far[np.random.randint(len(far))]
    return np.exp2(a.ravel()).repeat(32)


BF16 = ml_dtypes.bfloat16


def bf(x):
    return np.asarray(x, np.float32).astype(BF16)


def f64(x):
    return np.asarray(x).astype(np.float64)


E2M1 = np.array([0.0, 0.5, 1.0, 1.5, 2.0, 3.0, 4.0, 6.0, -0.0, -0.5, -1.0, -1.5, -2.0, -3.0, -4.0, -6.0])


def pack_weight(w, fmt):
    k, n = w.shape
    w = f64(bf(w)).reshape(k // 32, 32, n)
    amax = np.abs(w).max(1)
    if fmt == "e4m3":
        byte = np.frexp(amax)[1] - 1 + 127 - 7
    else:
        mant, ex = np.frexp(amax / 6.0)
        byte = np.where(mant > 0.5, ex, ex - 1) + 127
    byte = np.clip(np.where(amax > 0, byte, 1), 1, 254)
    scaled = (w * np.exp2(127.0 - byte)[:, None, :]).reshape(k, n).astype(np.float32)
    by_word = np.ascontiguousarray(scaled.reshape(k // 512, 128, 4, n).transpose(0, 1, 3, 2))
    if fmt == "e4m3":
        words = by_word.astype(ml_dtypes.float8_e4m3fn).view(np.uint8)
    else:
        c = by_word.astype(ml_dtypes.float4_e2m1fn).view(np.uint8) & 0xF
        words = c[..., 0::2] | (c[..., 1::2] << 4)
    return np.ascontiguousarray(words), np.ascontiguousarray(byte.astype(np.uint8).reshape(k // 512, 16, n))


def unpack_weight(words, scales, fmt):
    g, p, n, _ = words.shape
    if fmt == "e4m3":
        vals = np.ascontiguousarray(words).view(ml_dtypes.float8_e4m3fn).astype(np.float64)
    else:
        nib = np.empty((g, p, n, 4), np.uint8)
        nib[..., 0::2] = words & 0xF
        nib[..., 1::2] = words >> 4
        vals = E2M1[nib]
    vals = vals * np.repeat(np.exp2(scales.astype(np.float64) - 127.0), 8, axis=1)[..., None]
    return vals.transpose(0, 1, 3, 2).reshape(g * 512, n)
def pack4(w):
    words, scales = pack_weight(w, "e2m1")
    return words.reshape(words.shape[0], 128, -1), scales


def unpack4(words, scales):
    return unpack_weight(words.reshape(words.shape[0], 128, -1, 2), scales, "e2m1")


G, M, D, N = 4, 1024, 512, 1024


def setup_inputs():
    s = mx_kscale(G * D).reshape(G, D)
    t = mx_kscale(G * N).reshape(G, N)
    x = np.random.standard_normal((G, M, D))
    x = x / np.linalg.norm(x, axis=2, keepdims=True)
    b = np.random.standard_normal((G, N, D))
    b = b / np.linalg.norm(b, axis=2, keepdims=True)
    length = np.exp(0.3 * np.random.standard_normal((G, N)))
    a_words, a_scales = pack4((b.transpose(0, 2, 1) / s[:, :, None]).reshape(G * D, N))
    r_words, r_scales = pack4((b * (length / t)[:, :, None]).reshape(G * N, D))
    return {"x": bf(x * s[:, None, :]),
            "a_words": a_words, "a_scales": a_scales,
            "r_words": r_words, "r_scales": r_scales,
            "inv_norm": bf(t / length),
            "conc": bf(np.sqrt(D) * (0.5 + 0.3 * np.random.random(G)))}


def reference(x, a_words, a_scales, r_words, r_scales, inv_norm, conc):
    a = unpack4(a_words, a_scales).reshape(G, D, N)
    r = unpack4(r_words, r_scales).reshape(G, N, D)
    cos = mxq(f64(x), 2, "e4m3") @ a
    e = np.exp(f64(conc)[:, None, None] * cos)
    z = e.mean(axis=(1, 2), keepdims=True)
    w = e * f64(inv_norm)[:, None, :]
    return (mxq(w, 2, "e4m3") @ r) / z

@@ -1,0 +1,348 @@
+from contextlib import ExitStack
+
+import concourse.mybir as mybir
+from concourse.masks import make_identity
+
+G, M, D, N = 4, 1024, 512, 1024
+FLOPS = 2 * G * (M * D * N + M * N * D)
+
+F32 = mybir.dt.float32
+BF16 = mybir.dt.bfloat16
+I32 = mybir.dt.int32
+U32 = mybir.dt.uint32
+U8 = mybir.dt.uint8
+E4M3X4 = mybir.dt.float8_e4m3fn_x4
+E2M1X4 = mybir.dt.float4_e2m1fn_x4
+ACT = mybir.ActivationFunctionType
+ALU = mybir.AluOpType
+
+P = 128
+T = 4
+R = M // P
+HALF = 512
+NEIGHBOURS = 4
+VECTOR_OUT = (5, 9, 13, 15)
+
+
+def tile_sphere_uniformity_gradient_s14_kernel(
+    tc, x, a_words, a_scales, r_words, r_scales, inv_norm, conc, out
+):
+    nc = tc.nc
+    with ExitStack() as ctx:
+        keep = ctx.enter_context(tc.tile_pool(name="keep", bufs=1))
+        work = ctx.enter_context(tc.tile_pool(name="work", bufs=3))
+        psum = ctx.enter_context(tc.psum_pool(name="psum", bufs=2))
+        ctx.enter_context(tc.manual_schedule())
+
+        inv = keep.tile([P, 2 * G, T], BF16, name="inv", tag="inv")
+        conc_b = keep.tile([P, G], BF16, name="conc_b", tag="conc_b")
+        nc.scalar.dma_start(
+            out=inv[:], in_=inv_norm.rearrange("v n -> (v n)").rearrange("(a p t) -> p a t", p=P, t=T)
+        )
+        nc.scalar.dma_start(out=conc_b[:], in_=conc.partition_broadcast(P))
+
+        ident = keep.tile([P, P], F32, name="ident", tag="ident")
+        make_identity(nc, ident[:])
+
+        dummy = keep.tile([P, 1], F32, name="dummy", tag="dummy")
+        dummy2 = keep.tile([P, 1], F32, name="dummy2", tag="dummy2")
+        nc.vector.memset(dummy[:], 1.0)
+        mean_w = keep.tile([P, P], F32, name="mean_w", tag="mean_w")
+
+        a_raw_s = keep.tile([P, G, N], U8, name="a_raw_s", tag="a_raw_s", align_bytes=64)
+        r_s = keep.tile([P, 2 * G, D], U8, name="r_s", tag="r_s", align_bytes=64)
+        nc.vector.memset(a_raw_s[:].rearrange("p g n -> p (g n)").bitcast(I32), 0)
+        nc.gpsimd.memset(r_s[:].rearrange("p g n -> p (g n)").bitcast(I32), 0)
+        nc.vector.memset(mean_w[:], 1.0 / (M * N))
+
+        xb, aw, rw = {}, {}, {}
+        for v in range(G):
+            for h in range(2):
+                xb[v, h] = keep.tile([P, T, D], BF16, name=f"xb{v}{h}", tag=f"xb{v}{h}", align_bytes=64)
+            aw[v] = keep.tile([P, 2 * N], U8, name=f"aw{v}", tag=f"aw{v}", align_bytes=64)
+            rw[v] = keep.tile([P, 2, 2 * D], U8, name=f"rw{v}", tag=f"rw{v}", align_bytes=64)
+
+        def load_x(v, h, lo, hi):
+            rows = x[v].rearrange("(p r) k -> p r k", r=R)
+            nc.sync.dma_start(out=xb[v, h][:, lo:hi, :], in_=rows[:, 4 * h + lo : 4 * h + hi, :])
+
+        def load_a(v):
+            nc.sync.dma_start(out=aw[v][:].bitcast(I32), in_=a_words[v].bitcast(I32))
+
+        def load_r(v):
+            nc.sync.dma_start(
+                out=rw[v][:].bitcast(I32), in_=r_words[2 * v : 2 * v + 2].rearrange("g p n -> p g n").bitcast(I32)
+            )
+
+        def load_scales(plane, src):
+            for q in range(4):
+                nc.sync.dma_start(
+                    out=plane[32 * q : 32 * q + 4].bitcast(I32),
+                    in_=src[:, 4 * q : 4 * q + 4, :].rearrange("g q n -> q g n").bitcast(I32),
+                )
+
+        load_x(0, 0, 0, 2)
+        load_x(0, 0, 2, 4)
+        load_a(0)
+        load_scales(a_raw_s, a_scales)
+        load_x(0, 1, 0, 4)
+        load_a(1)
+        load_x(1, 0, 0, 4)
+        load_scales(r_s, r_scales)
+        load_r(0)
+        load_x(1, 1, 0, 4)
+        for v in range(1, G):
+            if v > 1:
+                load_x(v, 0, 0, 4)
+                load_x(v, 1, 0, 4)
+            if v + 1 < G:
+                load_a(v + 1)
+            load_r(v)
+
+        ln_inv = keep.tile([P, 2 * G * T], F32, name="ln_inv", tag="ln_inv")
+        conc_f = keep.tile([P, G], F32, name="conc_f", tag="conc_f")
+        rinv = keep.tile([P, G, 2, 2 * T], F32, name="rinv", tag="rinv")
+        nc.scalar.activation(out=dummy2[:], in_=dummy[:], func=ACT.Ln)
+        nc.scalar.activation(out=ln_inv[:], in_=inv[:].rearrange("p a t -> p (a t)"), func=ACT.Ln)
+        nc.scalar.activation(out=dummy2[:], in_=dummy[:], func=ACT.Exp)
+        nc.vector.tensor_copy(out=conc_f[:], in_=conc_b[:])
+        for h in range(2):
+            nc.vector.reciprocal(out=rinv[:, :, h, :], in_=inv[:].rearrange("p (v g) t -> p v (g t)", v=G))
+
+        ap_w, ap_s = {}, {}
+        for v in range(G):
+            ap_w[v] = keep.tile([P, 2, T, 2 * P], U8, name=f"apw{v}", tag=f"apw{v}", align_bytes=64)
+            ap_s[v] = keep.tile([P, 2, T, P], U8, name=f"aps{v}", tag=f"aps{v}", align_bytes=64)
+
+        def permute_words(v, g):
+            nc.vector.tensor_copy(
+                out=ap_w[v][:, g].rearrange("p t (m b) -> p t m b", b=2),
+                in_=aw[v][:, N * g : N * (g + 1)].rearrange("p (m t b) -> p t m b", t=T, b=2),
+            )
+
+        def permute_scales(v):
+            nc.vector.tensor_copy(
+                out=ap_s[v][:], in_=a_raw_s[:, v, :].rearrange("p (g m t) -> p g t m", g=2, t=T)
+            )
+
+        xt, xi, xq = {}, {}, {}
+
+        def transposes(v, h):
+            words = xb[v, h][:].rearrange("p r k -> p (r k)").bitcast(F32)
+            for b in range(2):
+                bank = psum.tile([P, 2, 2, P], F32, name="xt", tag="xt", bufs=2)
+                for r in range(2):
+                    for u in range(2):
+                        lo = (D // 2) * (2 * b + r)
+                        nc.tensor.transpose(bank[:, r, u, :], words[:, lo + u : lo + D // 2 : 2], ident[:])
+                xt[v, h, b] = bank
+            xi[v, h] = work.tile([P, HALF, T], BF16, name="xi", tag="xi", bufs=2, align_bytes=64)
+
+        def copy_x(v, h, b, engine):
+            dst = xi[v, h][:].rearrange("p m t -> p (m t)").bitcast(F32)
+            dst = dst[:, 512 * b : 512 * (b + 1)].rearrange("p (r m u) -> p r m u", r=2, u=2)
+            src = xt[v, h, b][:].rearrange("p r u m -> p r m u")
+            if engine == "vector":
+                nc.vector.tensor_copy(out=dst, in_=src)
+            else:
+                nc.scalar.copy(out=dst, in_=src)
+
+        def quantize_x(v, h):
+            codes = work.tile([P, HALF], U32, name="xc", tag="xc", bufs=3, align_bytes=64)
+            scales = work.tile([P, HALF], U8, name="xs", tag="xs", bufs=3, align_bytes=64)
+            nc.vector.quantize_mx(
+                out=codes[:].bitcast(E4M3X4), scales=scales[:], in_=xi[v, h][:].rearrange("p m t -> p (m t)")
+            )
+            xq[v, h] = (codes, scales)
+
+        def unit(u):
+            return u // 4, (u // 2) % 2, u % 2
+
+        cos, wr, wi, wq, sums = {}, {}, {}, {}, {}
+
+        def stage1(u, t):
+            v, h, g = unit(u)
+            codes, scales = xq[v, h]
+            bank = psum.tile([P, HALF], F32, name="cos", tag="cos", bufs=4)
+            nc.tensor.matmul_mx(
+                out=bank[:],
+                lhsT=ap_w[v][:, g, t, :].bitcast(E2M1X4),
+                lhsT_scale=ap_s[v][:, g, t, :],
+                rhs=codes[:].bitcast(E4M3X4),
+                rhs_scale=scales[:],
+                start=True,
+                stop=True,
+            )
+            cos[u, t] = bank
+
+        def exponentials(u, t):
+            v, h, g = unit(u)
+            if t == 0:
+                wr[u] = work.tile([P, T, HALF], BF16, name="wr", tag="wr", bufs=3, align_bytes=64)
+                if h == 0 and g == 0:
+                    sums[v] = keep.tile([P, 2, 2 * T], F32, name=f"sums{v}", tag=f"sums{v}")
+            j = (2 * v + g) * T + t
+            k = g * T + t
+            nc.scalar.activation(
+                out=wr[u][:, t, :],
+                in_=cos[u, t][:],
+                func=ACT.Exp,
+                bias=ln_inv[:, j : j + 1],
+                scale=conc_f[:, v : v + 1],
+                accum_out=sums[v][:, h, k : k + 1],
+            )
+
+        def interleave(u, lo=0, hi=HALF):
+            if lo == 0:
+                wi[u] = work.tile([P, HALF, T], BF16, name="wi", tag="wi", bufs=2, align_bytes=64)
+            nc.vector.tensor_copy(
+                out=wi[u][:, lo:hi, :].rearrange("p (c i) t -> p c t i", i=NEIGHBOURS),
+                in_=wr[u][:, :, lo:hi].rearrange("p t (c i) -> p c t i", i=NEIGHBOURS),
+            )
+
+        def quantize_w(u, lo=0, hi=HALF):
+            if lo == 0:
+                codes = work.tile([P, HALF], U32, name="wc", tag="wc", bufs=9, align_bytes=64)
+                scales = work.tile([P, HALF], U8, name="ws", tag="ws", bufs=9, align_bytes=64)
+                wq[u] = (codes, scales)
+            codes, scales = wq[u]
+            nc.vector.quantize_mx(
+                out=codes[:, lo:hi].bitcast(E4M3X4),
+                scales=scales[:, lo:hi],
+                in_=wi[u][:, lo:hi, :].rearrange("p m t -> p (m t)"),
+            )
+
+        rz = {}
+        zc = {}
+
+        def z_sum(v):
+            prod = work.tile([P, 2 * 2 * T], F32, name="prod", tag="prod", bufs=2)
+            zc[v] = work.tile([P, 1], F32, name="zc", tag="zc", bufs=2)
+            nc.vector.scalar_tensor_tensor(
+                out=prod[:],
+                in0=sums[v][:].rearrange("p h k -> p (h k)"),
+                scalar=1.0,
+                in1=rinv[:, v].rearrange("p h k -> p (h k)"),
+                op0=ALU.mult,
+                op1=ALU.mult,
+                accum_out=zc[v][:],
+            )
+
+        def z_mean(v, tag, bufs):
+            bank = psum.tile([P, 512], F32, name="zbank", tag=tag, bufs=bufs)
+            nc.tensor.matmul(out=bank[:, 0:1], lhsT=mean_w[:], rhs=zc[v][:], start=True, stop=True)
+            rz[v] = bank
+
+        def z_inverse(v):
+            r = keep.tile([P, 1], F32, name=f"rz{v}", tag=f"rz{v}")
+            nc.vector.reciprocal(out=r[:], in_=rz[v][:, 0:1])
+            rz[v] = r
+
+        grad = {}
+
+        def stage2(v, j, tag="grad", bufs=2, passes=(0, 1)):
+            h, r = j // 4, j % 4
+            if 0 in passes:
+                grad[v, j] = psum.tile([P, D], F32, name="grad", tag=tag, bufs=bufs)
+            for g in passes:
+                codes, scales = wq[4 * v + 2 * h + g]
+                nc.tensor.matmul_mx(
+                    out=grad[v, j][:],
+                    lhsT=codes[:, P * r : P * (r + 1)].bitcast(E4M3X4),
+                    lhsT_scale=scales[:, P * r : P * (r + 1)],
+                    rhs=rw[v][:, g, :].bitcast(E2M1X4),
+                    rhs_scale=r_s[:, 2 * v + g, :],
+                    start=(g == 0),
+                    stop=(g == 1),
+                )
+
+        def emit(v, j, engine):
+            o = work.tile([P, D], F32, name="o", tag="o", bufs=8)
+            if engine == "vector":
+                nc.vector.tensor_scalar(
+                    out=o[:], in0=grad[v, j][:], scalar1=rz[v][:, 0:1], scalar2=None, op0=ALU.mult
+                )
+            else:
+                nc.scalar.activation(out=o[:], in_=grad[v, j][:], func=ACT.Copy, scale=rz[v][:, 0:1])
+            nc.sync.dma_start(out=out[v].rearrange("(p r) d -> p r d", r=R)[:, j, :], in_=o[:])
+
+        transposes(0, 0)
+        copy_x(0, 0, 0, "vector")
+        copy_x(0, 0, 1, "vector")
+        permute_words(0, 0)
+        quantize_x(0, 0)
+        permute_scales(0)
+
+        units = 4 * G
+        for u in range(units):
+            v, h, g = unit(u)
+            prep = None
+            if u % 2 == 0 and u + 2 < units:
+                prep = unit(u + 2)[:2]
+            xeng = "scalar" if u < 4 else "vector"
+
+            stage1(u, 0)
+            exponentials(u, 0)
+            if v > 0 and u % 4 > 0:
+                emit(v - 1, 2 * (u % 4) - 1, "vector" if u in VECTOR_OUT else "scalar")
+            elif v > 1:
+                emit(v - 2, 7, "scalar")
+            stage1(u, 1)
+            exponentials(u, 1)
+            if u == 0:
+                permute_words(0, 1)
+            else:
+                if g == 0 and h == 0:
+                    z_sum(v - 1)
+                    z_mean(v - 1, "xt", 2)
+                interleave(u - 1)
+            if g == 0 and h == 0 and v > 0:
+                z_inverse(v - 1)
+            if g == 1:
+                pv, ph = unit(u + 1)[:2] if u + 1 < units else (None, None)
+                if pv is not None:
+                    quantize_x(pv, ph)
+            if v + 1 < G and u % 4 == 2:
+                permute_words(v + 1, 0)
+            if u > 0:
+                quantize_w(u - 1)
+            if v > 0:
+                stage2(v - 1, 2 * (u % 4))
+            stage1(u, 2)
+            exponentials(u, 2)
+            if v > 0:
+                emit(v - 1, 2 * (u % 4), "scalar")
+            if prep is not None:
+                transposes(*prep)
+            stage1(u, 3)
+            exponentials(u, 3)
+            if prep is not None:
+                copy_x(*prep, 0, xeng)
+                copy_x(*prep, 1, xeng)
+            if v + 1 < G and u % 4 == 1:
+                permute_scales(v + 1)
+            if v + 1 < G and u % 4 == 3:
+                permute_words(v + 1, 1)
+            if v > 0:
+                stage2(v - 1, 2 * (u % 4) + 1)
+
+        last = G - 1
+        emit(last - 1, 7, "vector")
+        stage2(last, 0, "xt", 2)
+        stage2(last, 1, "xt", 2)
+        stage2(last, 2)
+        z_sum(last)
+        z_mean(last, "cos", 4)
+        interleave(units - 1, 0, 256)
+        z_inverse(last)
+        stage2(last, 3)
+        for j in range(3):
+            emit(last, j, "scalar")
+        interleave(units - 1, 256, 512)
+        quantize_w(units - 1, 0, 256)
+        quantize_w(units - 1, 256, 512)
+        emit(last, 3, "scalar")
+        for j in range(4, 8):
+            stage2(last, j, "cos", 4)
+        for j in range(4, 8):
+            emit(last, j, "vector" if j % 2 == 0 else "scalar")

@@ -21,7 +21,9 @@ T = 4
 R = M // P
 HALF = 512
 NEIGHBOURS = 4
-VECTOR_OUT = (5, 9, 13, 15)
+TAIL_VECTOR = (1, 3, 5, 7)
+VECTOR_ODD = (14, 15)
+SCALAR_X = (0, 2)
 
 
 def tile_sphere_uniformity_gradient_s14_kernel(
@@ -39,19 +41,20 @@ def tile_sphere_uniformity_gradient_s14_kernel(
         nc.scalar.dma_start(
             out=inv[:], in_=inv_norm.rearrange("v n -> (v n)").rearrange("(a p t) -> p a t", p=P, t=T)
         )
-        nc.scalar.dma_start(out=conc_b[:], in_=conc.partition_broadcast(P))
-
         ident = keep.tile([P, P], F32, name="ident", tag="ident")
         make_identity(nc, ident[:])
+        nc.gpsimd.dma_start(out=conc_b[:], in_=conc.partition_broadcast(P))
 
         dummy = keep.tile([P, 1], F32, name="dummy", tag="dummy")
         dummy2 = keep.tile([P, 1], F32, name="dummy2", tag="dummy2")
         nc.vector.memset(dummy[:], 1.0)
         mean_w = keep.tile([P, P], F32, name="mean_w", tag="mean_w")
 
-        a_raw_s = keep.tile([P, G, N], U8, name="a_raw_s", tag="a_raw_s", align_bytes=64)
+        as_first = keep.tile([P, 1, N], U8, name="as_first", tag="as_first", align_bytes=64)
+        as_rest = keep.tile([P, G - 1, N], U8, name="as_rest", tag="as_rest", align_bytes=64)
         r_s = keep.tile([P, 2 * G, D], U8, name="r_s", tag="r_s", align_bytes=64)
-        nc.vector.memset(a_raw_s[:].rearrange("p g n -> p (g n)").bitcast(I32), 0)
+        nc.vector.memset(as_first[:].rearrange("p g n -> p (g n)").bitcast(I32), 0)
+        nc.vector.memset(as_rest[:].rearrange("p g n -> p (g n)").bitcast(I32), 0)
         nc.gpsimd.memset(r_s[:].rearrange("p g n -> p (g n)").bitcast(I32), 0)
         nc.vector.memset(mean_w[:], 1.0 / (M * N))
 
@@ -82,10 +85,11 @@ def tile_sphere_uniformity_gradient_s14_kernel(
                 )
 
         load_x(0, 0, 0, 2)
-        load_x(0, 0, 2, 4)
         load_a(0)
-        load_scales(a_raw_s, a_scales)
+        load_scales(as_first, a_scales[0:1])
+        load_x(0, 0, 2, 4)
         load_x(0, 1, 0, 4)
+        load_scales(as_rest, a_scales[1:G])
         load_a(1)
         load_x(1, 0, 0, 4)
         load_scales(r_s, r_scales)
@@ -101,12 +105,12 @@ def tile_sphere_uniformity_gradient_s14_kernel(
 
         ln_inv = keep.tile([P, 2 * G * T], F32, name="ln_inv", tag="ln_inv")
         conc_f = keep.tile([P, G], F32, name="conc_f", tag="conc_f")
-        rinv = keep.tile([P, G, 2, 2 * T], F32, name="rinv", tag="rinv")
+        rinv = keep.tile([P, G, 3, 2 * T], F32, name="rinv", tag="rinv")
         nc.scalar.activation(out=dummy2[:], in_=dummy[:], func=ACT.Ln)
         nc.scalar.activation(out=ln_inv[:], in_=inv[:].rearrange("p a t -> p (a t)"), func=ACT.Ln)
         nc.scalar.activation(out=dummy2[:], in_=dummy[:], func=ACT.Exp)
         nc.vector.tensor_copy(out=conc_f[:], in_=conc_b[:])
-        for h in range(2):
+        for h in range(3):
             nc.vector.reciprocal(out=rinv[:, :, h, :], in_=inv[:].rearrange("p (v g) t -> p v (g t)", v=G))
 
         ap_w, ap_s = {}, {}
@@ -120,23 +124,25 @@ def tile_sphere_uniformity_gradient_s14_kernel(
                 in_=aw[v][:, N * g : N * (g + 1)].rearrange("p (m t b) -> p t m b", t=T, b=2),
             )
 
-        def permute_scales(v):
+        def permute_scales(v, lo=0, hi=2):
+            src = as_first[:, 0, :] if v == 0 else as_rest[:, v - 1, :]
             nc.vector.tensor_copy(
-                out=ap_s[v][:], in_=a_raw_s[:, v, :].rearrange("p (g m t) -> p g t m", g=2, t=T)
+                out=ap_s[v][:, lo:hi], in_=src[:, 512 * lo : 512 * hi].rearrange("p (g m t) -> p g t m", m=P, t=T)
             )
 
         xt, xi, xq = {}, {}, {}
 
-        def transposes(v, h):
+        def transposes(v, h, banks=(0, 1)):
             words = xb[v, h][:].rearrange("p r k -> p (r k)").bitcast(F32)
-            for b in range(2):
+            for b in banks:
                 bank = psum.tile([P, 2, 2, P], F32, name="xt", tag="xt", bufs=2)
                 for r in range(2):
                     for u in range(2):
                         lo = (D // 2) * (2 * b + r)
                         nc.tensor.transpose(bank[:, r, u, :], words[:, lo + u : lo + D // 2 : 2], ident[:])
                 xt[v, h, b] = bank
-            xi[v, h] = work.tile([P, HALF, T], BF16, name="xi", tag="xi", bufs=2, align_bytes=64)
+            if 0 in banks:
+                xi[v, h] = work.tile([P, HALF, T], BF16, name="xi", tag="xi", bufs=2, align_bytes=64)
 
         def copy_x(v, h, b, engine):
             dst = xi[v, h][:].rearrange("p m t -> p (m t)").bitcast(F32)
@@ -147,49 +153,54 @@ def tile_sphere_uniformity_gradient_s14_kernel(
             else:
                 nc.scalar.copy(out=dst, in_=src)
 
-        def quantize_x(v, h):
-            codes = work.tile([P, HALF], U32, name="xc", tag="xc", bufs=3, align_bytes=64)
-            scales = work.tile([P, HALF], U8, name="xs", tag="xs", bufs=3, align_bytes=64)
+        def quantize_x(v, h, lo=0, hi=HALF):
+            if lo == 0:
+                codes = work.tile([P, HALF], U32, name="xc", tag="xc", bufs=3, align_bytes=64)
+                scales = work.tile([P, HALF], U8, name="xs", tag="xs", bufs=3, align_bytes=64)
+                xq[v, h] = (codes, scales)
+            codes, scales = xq[v, h]
             nc.vector.quantize_mx(
-                out=codes[:].bitcast(E4M3X4), scales=scales[:], in_=xi[v, h][:].rearrange("p m t -> p (m t)")
+                out=codes[:, lo:hi].bitcast(E4M3X4),
+                scales=scales[:, lo:hi],
+                in_=xi[v, h][:, lo:hi, :].rearrange("p m t -> p (m t)"),
             )
-            xq[v, h] = (codes, scales)
 
         def unit(u):
             return u // 4, (u // 2) % 2, u % 2
 
         cos, wr, wi, wq, sums = {}, {}, {}, {}, {}
 
-        def stage1(u, t):
+        def stage1(u, t, lo=0, hi=HALF):
             v, h, g = unit(u)
             codes, scales = xq[v, h]
             bank = psum.tile([P, HALF], F32, name="cos", tag="cos", bufs=4)
             nc.tensor.matmul_mx(
-                out=bank[:],
+                out=bank[:, 0 : hi - lo],
                 lhsT=ap_w[v][:, g, t, :].bitcast(E2M1X4),
                 lhsT_scale=ap_s[v][:, g, t, :],
-                rhs=codes[:].bitcast(E4M3X4),
-                rhs_scale=scales[:],
+                rhs=codes[:, lo:hi].bitcast(E4M3X4),
+                rhs_scale=scales[:, lo:hi],
                 start=True,
                 stop=True,
             )
-            cos[u, t] = bank
+            cos[u, t, lo] = bank
 
-        def exponentials(u, t):
+        def exponentials(u, t, lo=0, hi=HALF):
             v, h, g = unit(u)
-            if t == 0:
+            if t == 0 and lo == 0:
                 wr[u] = work.tile([P, T, HALF], BF16, name="wr", tag="wr", bufs=3, align_bytes=64)
                 if h == 0 and g == 0:
-                    sums[v] = keep.tile([P, 2, 2 * T], F32, name=f"sums{v}", tag=f"sums{v}")
+                    sums[v] = keep.tile([P, 3, 2 * T], F32, name=f"sums{v}", tag=f"sums{v}")
+                    nc.vector.memset(sums[v][:, 2, :], 0.0)
             j = (2 * v + g) * T + t
             k = g * T + t
             nc.scalar.activation(
-                out=wr[u][:, t, :],
-                in_=cos[u, t][:],
+                out=wr[u][:, t, lo:hi],
+                in_=cos[u, t, lo][:, 0 : hi - lo],
                 func=ACT.Exp,
                 bias=ln_inv[:, j : j + 1],
                 scale=conc_f[:, v : v + 1],
-                accum_out=sums[v][:, h, k : k + 1],
+                accum_out=sums[v][:, h if lo == 0 else 2, k : k + 1],
             )
 
         def interleave(u, lo=0, hi=HALF):
@@ -216,7 +227,7 @@ def tile_sphere_uniformity_gradient_s14_kernel(
         zc = {}
 
         def z_sum(v):
-            prod = work.tile([P, 2 * 2 * T], F32, name="prod", tag="prod", bufs=2)
+            prod = work.tile([P, 3 * 2 * T], F32, name="prod", tag="prod", bufs=2)
             zc[v] = work.tile([P, 1], F32, name="zc", tag="zc", bufs=2)
             nc.vector.scalar_tensor_tensor(
                 out=prod[:],
@@ -266,83 +277,102 @@ def tile_sphere_uniformity_gradient_s14_kernel(
                 nc.scalar.activation(out=o[:], in_=grad[v, j][:], func=ACT.Copy, scale=rz[v][:, 0:1])
             nc.sync.dma_start(out=out[v].rearrange("(p r) d -> p r d", r=R)[:, j, :], in_=o[:])
 
-        transposes(0, 0)
-        copy_x(0, 0, 0, "vector")
-        copy_x(0, 0, 1, "vector")
-        permute_words(0, 0)
-        quantize_x(0, 0)
-        permute_scales(0)
-
         units = 4 * G
+        last = G - 1
+        transposes(0, 0, (0,))
+        copy_x(0, 0, 0, "vector")
+        permute_words(0, 0)
+        permute_scales(0, 0, 1)
+        quantize_x(0, 0, 0, 256)
+        transposes(0, 0, (1,))
+        copy_x(0, 0, 1, "vector")
+        for t in range(T):
+            stage1(0, t, 0, 256)
+            exponentials(0, t, 0, 256)
+        quantize_x(0, 0, 256, 512)
+        transposes(0, 1)
+        permute_words(0, 1)
+        permute_scales(0, 1, 2)
+
         for u in range(units):
             v, h, g = unit(u)
-            prep = None
-            if u % 2 == 0 and u + 2 < units:
-                prep = unit(u + 2)[:2]
-            xeng = "scalar" if u < 4 else "vector"
+            first = v > 0 and u % 4 == 0
+            even, odd = 2 * (u % 4), 2 * (u % 4) + 1
+            final = u == units - 1
+            prep = unit(u + 2)[:2] if g == 0 and u + 2 < units else None
+            later = unit(u + 3)[:2] if g == 1 and u + 3 < units else None
+            before = (v - 1, odd - 2) if v > 0 and not first else ((v - 2, 7) if v > 1 else None)
+            c = (256, 512) if u == 0 or final else (0, 512)
 
-            stage1(u, 0)
-            exponentials(u, 0)
-            if v > 0 and u % 4 > 0:
-                emit(v - 1, 2 * (u % 4) - 1, "vector" if u in VECTOR_OUT else "scalar")
-            elif v > 1:
-                emit(v - 2, 7, "scalar")
-            stage1(u, 1)
-            exponentials(u, 1)
-            if u == 0:
-                permute_words(0, 1)
-            else:
-                if g == 0 and h == 0:
-                    z_sum(v - 1)
-                    z_mean(v - 1, "xt", 2)
+            if first:
+                z_sum(v - 1)
+            if u > 0:
                 interleave(u - 1)
-            if g == 0 and h == 0 and v > 0:
-                z_inverse(v - 1)
-            if g == 1:
-                pv, ph = unit(u + 1)[:2] if u + 1 < units else (None, None)
-                if pv is not None:
-                    quantize_x(pv, ph)
             if v + 1 < G and u % 4 == 2:
-                permute_words(v + 1, 0)
+                permute_scales(v + 1)
+            if prep is not None and u in SCALAR_X:
+                copy_x(*prep, 0, "scalar")
+
+            if final:
+                for t in range(T):
+                    stage1(u, t, 0, 256)
+                    exponentials(u, t, 0, 256)
+                    if t == 0:
+                        stage2(*before)
+                        emit(*before, "vector" if u in VECTOR_ODD else "scalar")
+            stage1(u, 0, *c)
+            exponentials(u, 0, *c)
+            if before is not None and not final:
+                stage2(*before)
+                emit(*before, "vector" if u in VECTOR_ODD else "scalar")
+            stage1(u, 1, *c)
+            exponentials(u, 1, *c)
+            stage1(u, 2, *c)
+            exponentials(u, 2, *c)
+            if v > 0 and not first:
+                stage2(v - 1, even)
+                if not final:
+                    emit(v - 1, even, "vector" if g == 1 else "scalar")
+            stage1(u, 3, *c)
+            exponentials(u, 3, *c)
+            if first:
+                z_mean(v - 1, "grad", 2)
+                z_inverse(v - 1)
+                stage2(v - 1, even)
+                emit(v - 1, even, "scalar")
+            if prep is not None:
+                if u not in SCALAR_X:
+                    copy_x(*prep, 0, "vector")
+                copy_x(*prep, 1, "vector")
+            if later is not None:
+                transposes(*later)
             if u > 0:
                 quantize_w(u - 1)
-            if v > 0:
-                stage2(v - 1, 2 * (u % 4))
-            stage1(u, 2)
-            exponentials(u, 2)
-            if v > 0:
-                emit(v - 1, 2 * (u % 4), "scalar")
             if prep is not None:
-                transposes(*prep)
-            stage1(u, 3)
-            exponentials(u, 3)
-            if prep is not None:
-                copy_x(*prep, 0, xeng)
-                copy_x(*prep, 1, xeng)
+                quantize_x(*prep)
             if v + 1 < G and u % 4 == 1:
-                permute_scales(v + 1)
+                permute_words(v + 1, 0)
             if v + 1 < G and u % 4 == 3:
                 permute_words(v + 1, 1)
-            if v > 0:
-                stage2(v - 1, 2 * (u % 4) + 1)
 
-        last = G - 1
-        emit(last - 1, 7, "vector")
+        u = units - 1
+        interleave(u, 0, 256)
+        emit(last - 1, 6, "vector")
+        quantize_w(u, 0, 256)
+        stage2(last - 1, 7)
+        emit(last - 1, 7, "scalar")
         stage2(last, 0, "xt", 2)
         stage2(last, 1, "xt", 2)
-        stage2(last, 2)
         z_sum(last)
         z_mean(last, "cos", 4)
-        interleave(units - 1, 0, 256)
+        interleave(u, 256, 512)
         z_inverse(last)
+        quantize_w(u, 256, 512)
+        stage2(last, 2)
         stage2(last, 3)
-        for j in range(3):
-            emit(last, j, "scalar")
-        interleave(units - 1, 256, 512)
-        quantize_w(units - 1, 0, 256)
-        quantize_w(units - 1, 256, 512)
-        emit(last, 3, "scalar")
-        for j in range(4, 8):
-            stage2(last, j, "cos", 4)
-        for j in range(4, 8):
-            emit(last, j, "vector" if j % 2 == 0 else "scalar")
+        stage2(last, 4, "cos", 4)
+        stage2(last, 5, "cos", 4)
+        stage2(last, 6, "cos", 4)
+        stage2(last, 7, "cos", 4)
+        for j in range(8):
+            emit(last, j, "vector" if j in TAIL_VECTOR else "scalar")

@@ -43,7 +43,7 @@ def tile_sphere_uniformity_gradient_s14_kernel(
         )
         ident = keep.tile([P, P], F32, name="ident", tag="ident")
         make_identity(nc, ident[:])
-        nc.gpsimd.dma_start(out=conc_b[:], in_=conc.partition_broadcast(P))
+        nc.scalar.dma_start(out=conc_b[:], in_=conc.partition_broadcast(P))
 
         dummy = keep.tile([P, 1], F32, name="dummy", tag="dummy")
         dummy2 = keep.tile([P, 1], F32, name="dummy2", tag="dummy2")
@@ -55,7 +55,7 @@ def tile_sphere_uniformity_gradient_s14_kernel(
         r_s = keep.tile([P, 2 * G, D], U8, name="r_s", tag="r_s", align_bytes=64)
         nc.vector.memset(as_first[:].rearrange("p g n -> p (g n)").bitcast(I32), 0)
         nc.vector.memset(as_rest[:].rearrange("p g n -> p (g n)").bitcast(I32), 0)
-        nc.gpsimd.memset(r_s[:].rearrange("p g n -> p (g n)").bitcast(I32), 0)
+        nc.vector.memset(r_s[:].rearrange("p g n -> p (g n)").bitcast(I32), 0)
         nc.vector.memset(mean_w[:], 1.0 / (M * N))
 
         xb, aw, rw = {}, {}, {}
@@ -109,9 +109,11 @@ def tile_sphere_uniformity_gradient_s14_kernel(
         nc.scalar.activation(out=dummy2[:], in_=dummy[:], func=ACT.Ln)
         nc.scalar.activation(out=ln_inv[:], in_=inv[:].rearrange("p a t -> p (a t)"), func=ACT.Ln)
         nc.scalar.activation(out=dummy2[:], in_=dummy[:], func=ACT.Exp)
-        nc.vector.tensor_copy(out=conc_f[:], in_=conc_b[:])
-        for h in range(3):
-            nc.vector.reciprocal(out=rinv[:, :, h, :], in_=inv[:].rearrange("p (v g) t -> p v (g t)", v=G))
+
+        def small_vectors():
+            nc.vector.tensor_copy(out=conc_f[:], in_=conc_b[:])
+            for h in range(3):
+                nc.vector.reciprocal(out=rinv[:, :, h, :], in_=inv[:].rearrange("p (v g) t -> p v (g t)", v=G))
 
         ap_w, ap_s = {}, {}
         for v in range(G):
@@ -249,7 +251,7 @@ def tile_sphere_uniformity_gradient_s14_kernel(
             nc.vector.reciprocal(out=r[:], in_=rz[v][:, 0:1])
             rz[v] = r
 
-        grad = {}
+        grad, pairs = {}, {}
 
         def stage2(v, j, tag="grad", bufs=2, passes=(0, 1)):
             h, r = j // 4, j % 4
@@ -268,14 +270,19 @@ def tile_sphere_uniformity_gradient_s14_kernel(
                 )
 
         def emit(v, j, engine):
-            o = work.tile([P, D], F32, name="o", tag="o", bufs=8)
+            if j % 2 == 0:
+                pairs[v, j // 2] = work.tile([P, 2, D], F32, name="o", tag="o", bufs=5)
+            o = pairs[v, j // 2][:, j % 2, :]
             if engine == "vector":
                 nc.vector.tensor_scalar(
-                    out=o[:], in0=grad[v, j][:], scalar1=rz[v][:, 0:1], scalar2=None, op0=ALU.mult
+                    out=o, in0=grad[v, j][:], scalar1=rz[v][:, 0:1], scalar2=None, op0=ALU.mult
                 )
             else:
-                nc.scalar.activation(out=o[:], in_=grad[v, j][:], func=ACT.Copy, scale=rz[v][:, 0:1])
-            nc.sync.dma_start(out=out[v].rearrange("(p r) d -> p r d", r=R)[:, j, :], in_=o[:])
+                nc.scalar.activation(out=o, in_=grad[v, j][:], func=ACT.Copy, scale=rz[v][:, 0:1])
+            if j % 2 == 1:
+                nc.sync.dma_start(
+                    out=out[v].rearrange("(p r) d -> p r d", r=R)[:, j - 1 : j + 1, :], in_=pairs[v, j // 2][:]
+                )
 
         units = 4 * G
         last = G - 1
@@ -284,6 +291,7 @@ def tile_sphere_uniformity_gradient_s14_kernel(
         permute_words(0, 0)
         permute_scales(0, 0, 1)
         quantize_x(0, 0, 0, 256)
+        small_vectors()
         transposes(0, 0, (1,))
         copy_x(0, 0, 1, "vector")
         for t in range(T):
@@ -346,14 +354,14 @@ def tile_sphere_uniformity_gradient_s14_kernel(
                 copy_x(*prep, 1, "vector")
             if later is not None:
                 transposes(*later)
-            if u > 0:
-                quantize_w(u - 1)
-            if prep is not None:
-                quantize_x(*prep)
             if v + 1 < G and u % 4 == 1:
                 permute_words(v + 1, 0)
             if v + 1 < G and u % 4 == 3:
                 permute_words(v + 1, 1)
+            if u > 0:
+                quantize_w(u - 1)
+            if prep is not None:
+                quantize_x(*prep)
 
         u = units - 1
         interleave(u, 0, 256)

from contextlib import ExitStack

import concourse.mybir as mybir
from concourse.masks import make_identity

G, M, D, N = 4, 1024, 512, 1024
FLOPS = 2 * G * (M * D * N + M * N * D)

F32 = mybir.dt.float32
BF16 = mybir.dt.bfloat16
I32 = mybir.dt.int32
U32 = mybir.dt.uint32
U8 = mybir.dt.uint8
E4M3X4 = mybir.dt.float8_e4m3fn_x4
E2M1X4 = mybir.dt.float4_e2m1fn_x4
ACT = mybir.ActivationFunctionType
ALU = mybir.AluOpType

P = 128
T = 4
R = M // P
HALF = 512
NEIGHBOURS = 4
TAIL_VECTOR = (1, 3, 5, 7)
VECTOR_ODD = (14, 15)
SCALAR_X = (0, 2)


def tile_sphere_uniformity_gradient_s14_kernel(
    tc, x, a_words, a_scales, r_words, r_scales, inv_norm, conc, out
):
    nc = tc.nc
    with ExitStack() as ctx:
        keep = ctx.enter_context(tc.tile_pool(name="keep", bufs=1))
        work = ctx.enter_context(tc.tile_pool(name="work", bufs=3))
        psum = ctx.enter_context(tc.psum_pool(name="psum", bufs=2))
        ctx.enter_context(tc.manual_schedule())

        inv = keep.tile([P, 2 * G, T], BF16, name="inv", tag="inv")
        conc_b = keep.tile([P, G], BF16, name="conc_b", tag="conc_b")
        nc.scalar.dma_start(
            out=inv[:], in_=inv_norm.rearrange("v n -> (v n)").rearrange("(a p t) -> p a t", p=P, t=T)
        )
        ident = keep.tile([P, P], F32, name="ident", tag="ident")
        make_identity(nc, ident[:])
        nc.scalar.dma_start(out=conc_b[:], in_=conc.partition_broadcast(P))

        dummy = keep.tile([P, 1], F32, name="dummy", tag="dummy")
        dummy2 = keep.tile([P, 1], F32, name="dummy2", tag="dummy2")
        nc.vector.memset(dummy[:], 1.0)
        mean_w = keep.tile([P, P], F32, name="mean_w", tag="mean_w")

        as_first = keep.tile([P, 1, N], U8, name="as_first", tag="as_first", align_bytes=64)
        as_rest = keep.tile([P, G - 1, N], U8, name="as_rest", tag="as_rest", align_bytes=64)
        r_s = keep.tile([P, 2 * G, D], U8, name="r_s", tag="r_s", align_bytes=64)
        nc.vector.memset(as_first[:].rearrange("p g n -> p (g n)").bitcast(I32), 0)
        nc.vector.memset(as_rest[:].rearrange("p g n -> p (g n)").bitcast(I32), 0)
        nc.vector.memset(r_s[:].rearrange("p g n -> p (g n)").bitcast(I32), 0)
        nc.vector.memset(mean_w[:], 1.0 / (M * N))

        xb, aw, rw = {}, {}, {}
        for v in range(G):
            for h in range(2):
                xb[v, h] = keep.tile([P, T, D], BF16, name=f"xb{v}{h}", tag=f"xb{v}{h}", align_bytes=64)
            aw[v] = keep.tile([P, 2 * N], U8, name=f"aw{v}", tag=f"aw{v}", align_bytes=64)
            rw[v] = keep.tile([P, 2, 2 * D], U8, name=f"rw{v}", tag=f"rw{v}", align_bytes=64)

        def load_x(v, h, lo, hi):
            rows = x[v].rearrange("(p r) k -> p r k", r=R)
            nc.sync.dma_start(out=xb[v, h][:, lo:hi, :], in_=rows[:, 4 * h + lo : 4 * h + hi, :])

        def load_a(v):
            nc.sync.dma_start(out=aw[v][:].bitcast(I32), in_=a_words[v].bitcast(I32))

        def load_r(v):
            nc.sync.dma_start(
                out=rw[v][:].bitcast(I32), in_=r_words[2 * v : 2 * v + 2].rearrange("g p n -> p g n").bitcast(I32)
            )

        def load_scales(plane, src):
            for q in range(4):
                nc.sync.dma_start(
                    out=plane[32 * q : 32 * q + 4].bitcast(I32),
                    in_=src[:, 4 * q : 4 * q + 4, :].rearrange("g q n -> q g n").bitcast(I32),
                )

        load_x(0, 0, 0, 2)
        load_a(0)
        load_scales(as_first, a_scales[0:1])
        load_x(0, 0, 2, 4)
        load_x(0, 1, 0, 4)
        load_scales(as_rest, a_scales[1:G])
        load_a(1)
        load_x(1, 0, 0, 4)
        load_scales(r_s, r_scales)
        load_r(0)
        load_x(1, 1, 0, 4)
        for v in range(1, G):
            if v > 1:
                load_x(v, 0, 0, 4)
                load_x(v, 1, 0, 4)
            if v + 1 < G:
                load_a(v + 1)
            load_r(v)

        ln_inv = keep.tile([P, 2 * G * T], F32, name="ln_inv", tag="ln_inv")
        conc_f = keep.tile([P, G], F32, name="conc_f", tag="conc_f")
        rinv = keep.tile([P, G, 3, 2 * T], F32, name="rinv", tag="rinv")
        nc.scalar.activation(out=dummy2[:], in_=dummy[:], func=ACT.Ln)
        nc.scalar.activation(out=ln_inv[:], in_=inv[:].rearrange("p a t -> p (a t)"), func=ACT.Ln)
        nc.scalar.activation(out=dummy2[:], in_=dummy[:], func=ACT.Exp)

        def small_vectors():
            nc.vector.tensor_copy(out=conc_f[:], in_=conc_b[:])
            for h in range(3):
                nc.vector.reciprocal(out=rinv[:, :, h, :], in_=inv[:].rearrange("p (v g) t -> p v (g t)", v=G))

        ap_w, ap_s = {}, {}
        for v in range(G):
            ap_w[v] = keep.tile([P, 2, T, 2 * P], U8, name=f"apw{v}", tag=f"apw{v}", align_bytes=64)
            ap_s[v] = keep.tile([P, 2, T, P], U8, name=f"aps{v}", tag=f"aps{v}", align_bytes=64)

        def permute_words(v, g):
            nc.vector.tensor_copy(
                out=ap_w[v][:, g].rearrange("p t (m b) -> p t m b", b=2),
                in_=aw[v][:, N * g : N * (g + 1)].rearrange("p (m t b) -> p t m b", t=T, b=2),
            )

        def permute_scales(v, lo=0, hi=2):
            src = as_first[:, 0, :] if v == 0 else as_rest[:, v - 1, :]
            nc.vector.tensor_copy(
                out=ap_s[v][:, lo:hi], in_=src[:, 512 * lo : 512 * hi].rearrange("p (g m t) -> p g t m", m=P, t=T)
            )

        xt, xi, xq = {}, {}, {}

        def transposes(v, h, banks=(0, 1)):
            words = xb[v, h][:].rearrange("p r k -> p (r k)").bitcast(F32)
            for b in banks:
                bank = psum.tile([P, 2, 2, P], F32, name="xt", tag="xt", bufs=2)
                for r in range(2):
                    for u in range(2):
                        lo = (D // 2) * (2 * b + r)
                        nc.tensor.transpose(bank[:, r, u, :], words[:, lo + u : lo + D // 2 : 2], ident[:])
                xt[v, h, b] = bank
            if 0 in banks:
                xi[v, h] = work.tile([P, HALF, T], BF16, name="xi", tag="xi", bufs=2, align_bytes=64)

        def copy_x(v, h, b, engine):
            dst = xi[v, h][:].rearrange("p m t -> p (m t)").bitcast(F32)
            dst = dst[:, 512 * b : 512 * (b + 1)].rearrange("p (r m u) -> p r m u", r=2, u=2)
            src = xt[v, h, b][:].rearrange("p r u m -> p r m u")
            if engine == "vector":
                nc.vector.tensor_copy(out=dst, in_=src)
            else:
                nc.scalar.copy(out=dst, in_=src)

        def quantize_x(v, h, lo=0, hi=HALF):
            if lo == 0:
                codes = work.tile([P, HALF], U32, name="xc", tag="xc", bufs=3, align_bytes=64)
                scales = work.tile([P, HALF], U8, name="xs", tag="xs", bufs=3, align_bytes=64)
                xq[v, h] = (codes, scales)
            codes, scales = xq[v, h]
            nc.vector.quantize_mx(
                out=codes[:, lo:hi].bitcast(E4M3X4),
                scales=scales[:, lo:hi],
                in_=xi[v, h][:, lo:hi, :].rearrange("p m t -> p (m t)"),
            )

        def unit(u):
            return u // 4, (u // 2) % 2, u % 2

        cos, wr, wi, wq, sums = {}, {}, {}, {}, {}

        def stage1(u, t, lo=0, hi=HALF):
            v, h, g = unit(u)
            codes, scales = xq[v, h]
            bank = psum.tile([P, HALF], F32, name="cos", tag="cos", bufs=4)
            nc.tensor.matmul_mx(
                out=bank[:, 0 : hi - lo],
                lhsT=ap_w[v][:, g, t, :].bitcast(E2M1X4),
                lhsT_scale=ap_s[v][:, g, t, :],
                rhs=codes[:, lo:hi].bitcast(E4M3X4),
                rhs_scale=scales[:, lo:hi],
                start=True,
                stop=True,
            )
            cos[u, t, lo] = bank

        def exponentials(u, t, lo=0, hi=HALF):
            v, h, g = unit(u)
            if t == 0 and lo == 0:
                wr[u] = work.tile([P, T, HALF], BF16, name="wr", tag="wr", bufs=3, align_bytes=64)
                if h == 0 and g == 0:
                    sums[v] = keep.tile([P, 3, 2 * T], F32, name=f"sums{v}", tag=f"sums{v}")
                    nc.vector.memset(sums[v][:, 2, :], 0.0)
            j = (2 * v + g) * T + t
            k = g * T + t
            nc.scalar.activation(
                out=wr[u][:, t, lo:hi],
                in_=cos[u, t, lo][:, 0 : hi - lo],
                func=ACT.Exp,
                bias=ln_inv[:, j : j + 1],
                scale=conc_f[:, v : v + 1],
                accum_out=sums[v][:, h if lo == 0 else 2, k : k + 1],
            )

        def interleave(u, lo=0, hi=HALF):
            if lo == 0:
                wi[u] = work.tile([P, HALF, T], BF16, name="wi", tag="wi", bufs=2, align_bytes=64)
            nc.vector.tensor_copy(
                out=wi[u][:, lo:hi, :].rearrange("p (c i) t -> p c t i", i=NEIGHBOURS),
                in_=wr[u][:, :, lo:hi].rearrange("p t (c i) -> p c t i", i=NEIGHBOURS),
            )

        def quantize_w(u, lo=0, hi=HALF):
            if lo == 0:
                codes = work.tile([P, HALF], U32, name="wc", tag="wc", bufs=9, align_bytes=64)
                scales = work.tile([P, HALF], U8, name="ws", tag="ws", bufs=9, align_bytes=64)
                wq[u] = (codes, scales)
            codes, scales = wq[u]
            nc.vector.quantize_mx(
                out=codes[:, lo:hi].bitcast(E4M3X4),
                scales=scales[:, lo:hi],
                in_=wi[u][:, lo:hi, :].rearrange("p m t -> p (m t)"),
            )

        rz = {}
        zc = {}

        def z_sum(v):
            prod = work.tile([P, 3 * 2 * T], F32, name="prod", tag="prod", bufs=2)
            zc[v] = work.tile([P, 1], F32, name="zc", tag="zc", bufs=2)
            nc.vector.scalar_tensor_tensor(
                out=prod[:],
                in0=sums[v][:].rearrange("p h k -> p (h k)"),
                scalar=1.0,
                in1=rinv[:, v].rearrange("p h k -> p (h k)"),
                op0=ALU.mult,
                op1=ALU.mult,
                accum_out=zc[v][:],
            )

        def z_mean(v, tag, bufs):
            bank = psum.tile([P, 512], F32, name="zbank", tag=tag, bufs=bufs)
            nc.tensor.matmul(out=bank[:, 0:1], lhsT=mean_w[:], rhs=zc[v][:], start=True, stop=True)
            rz[v] = bank

        def z_inverse(v):
            r = keep.tile([P, 1], F32, name=f"rz{v}", tag=f"rz{v}")
            nc.vector.reciprocal(out=r[:], in_=rz[v][:, 0:1])
            rz[v] = r

        grad, pairs = {}, {}

        def stage2(v, j, tag="grad", bufs=2, passes=(0, 1)):
            h, r = j // 4, j % 4
            if 0 in passes:
                grad[v, j] = psum.tile([P, D], F32, name="grad", tag=tag, bufs=bufs)
            for g in passes:
                codes, scales = wq[4 * v + 2 * h + g]
                nc.tensor.matmul_mx(
                    out=grad[v, j][:],
                    lhsT=codes[:, P * r : P * (r + 1)].bitcast(E4M3X4),
                    lhsT_scale=scales[:, P * r : P * (r + 1)],
                    rhs=rw[v][:, g, :].bitcast(E2M1X4),
                    rhs_scale=r_s[:, 2 * v + g, :],
                    start=(g == 0),
                    stop=(g == 1),
                )

        def emit(v, j, engine):
            if j % 2 == 0:
                pairs[v, j // 2] = work.tile([P, 2, D], F32, name="o", tag="o", bufs=5)
            o = pairs[v, j // 2][:, j % 2, :]
            if engine == "vector":
                nc.vector.tensor_scalar(
                    out=o, in0=grad[v, j][:], scalar1=rz[v][:, 0:1], scalar2=None, op0=ALU.mult
                )
            else:
                nc.scalar.activation(out=o, in_=grad[v, j][:], func=ACT.Copy, scale=rz[v][:, 0:1])
            if j % 2 == 1:
                nc.sync.dma_start(
                    out=out[v].rearrange("(p r) d -> p r d", r=R)[:, j - 1 : j + 1, :], in_=pairs[v, j // 2][:]
                )

        units = 4 * G
        last = G - 1
        transposes(0, 0, (0,))
        copy_x(0, 0, 0, "vector")
        permute_words(0, 0)
        permute_scales(0, 0, 1)
        quantize_x(0, 0, 0, 256)
        small_vectors()
        transposes(0, 0, (1,))
        copy_x(0, 0, 1, "vector")
        for t in range(T):
            stage1(0, t, 0, 256)
            exponentials(0, t, 0, 256)
        quantize_x(0, 0, 256, 512)
        transposes(0, 1)
        permute_words(0, 1)
        permute_scales(0, 1, 2)

        for u in range(units):
            v, h, g = unit(u)
            first = v > 0 and u % 4 == 0
            even, odd = 2 * (u % 4), 2 * (u % 4) + 1
            final = u == units - 1
            prep = unit(u + 2)[:2] if g == 0 and u + 2 < units else None
            later = unit(u + 3)[:2] if g == 1 and u + 3 < units else None
            before = (v - 1, odd - 2) if v > 0 and not first else ((v - 2, 7) if v > 1 else None)
            c = (256, 512) if u == 0 or final else (0, 512)

            if first:
                z_sum(v - 1)
            if u > 0:
                interleave(u - 1)
            if v + 1 < G and u % 4 == 2:
                permute_scales(v + 1)
            if prep is not None and u in SCALAR_X:
                copy_x(*prep, 0, "scalar")

            if final:
                for t in range(T):
                    stage1(u, t, 0, 256)
                    exponentials(u, t, 0, 256)
                    if t == 0:
                        stage2(*before)
                        emit(*before, "vector" if u in VECTOR_ODD else "scalar")
            stage1(u, 0, *c)
            exponentials(u, 0, *c)
            if before is not None and not final:
                stage2(*before)
                emit(*before, "vector" if u in VECTOR_ODD else "scalar")
            stage1(u, 1, *c)
            exponentials(u, 1, *c)
            stage1(u, 2, *c)
            exponentials(u, 2, *c)
            if v > 0 and not first:
                stage2(v - 1, even)
                if not final:
                    emit(v - 1, even, "vector" if g == 1 else "scalar")
            stage1(u, 3, *c)
            exponentials(u, 3, *c)
            if first:
                z_mean(v - 1, "grad", 2)
                z_inverse(v - 1)
                stage2(v - 1, even)
                emit(v - 1, even, "scalar")
            if prep is not None:
                if u not in SCALAR_X:
                    copy_x(*prep, 0, "vector")
                copy_x(*prep, 1, "vector")
            if later is not None:
                transposes(*later)
            if v + 1 < G and u % 4 == 1:
                permute_words(v + 1, 0)
            if v + 1 < G and u % 4 == 3:
                permute_words(v + 1, 1)
            if u > 0:
                quantize_w(u - 1)
            if prep is not None:
                quantize_x(*prep)

        u = units - 1
        interleave(u, 0, 256)
        emit(last - 1, 6, "vector")
        quantize_w(u, 0, 256)
        stage2(last - 1, 7)
        emit(last - 1, 7, "scalar")
        stage2(last, 0, "xt", 2)
        stage2(last, 1, "xt", 2)
        z_sum(last)
        z_mean(last, "cos", 4)
        interleave(u, 256, 512)
        z_inverse(last)
        quantize_w(u, 256, 512)
        stage2(last, 2)
        stage2(last, 3)
        stage2(last, 4, "cos", 4)
        stage2(last, 5, "cos", 4)
        stage2(last, 6, "cos", 4)
        stage2(last, 7, "cos", 4)
        for j in range(8):
            emit(last, j, "vector" if j in TAIL_VECTOR else "scalar")
